import numpy as np
import ml_dtypes


def mxq(x, axis, fmt="e4m3"):
    dtype, down = {"e4m3": (ml_dtypes.float8_e4m3fn, 7), "e5m2": (ml_dtypes.float8_e5m2, 14)}[fmt]
    v = np.moveaxis(np.asarray(x, np.float32).astype(ml_dtypes.bfloat16).astype(np.float64), axis, -1)
    blocks = v.reshape(v.shape[:-1] + (-1, 32))
    amax = np.abs(blocks).max(-1, keepdims=True)
    byte = np.maximum(np.where(amax > 0, np.frexp(amax)[1] - 1 + 127, 0) - down, 1)
    scale = np.exp2(byte - 127.0)
    codes = (blocks / scale).astype(np.float32).astype(dtype).astype(np.float64)
    return np.moveaxis((codes * scale).reshape(v.shape), -1, axis)


WIDE = False


def mx_kscale(k):
    if not WIDE:
        return np.ones(k)
    levels = np.array([10, -10, 5, -5, 0])
    if k % 512:
        return np.exp2(np.random.permutation(np.resize(levels, k // 32))).repeat(32)
    a = np.empty((k // 512, 16))
    for p in range(k // 512):
        a[p, :8] = np.random.permutation(np.resize(levels, 8))
        for g in range(8):
            far = levels[np.abs(levels - a[p, g]) >= 10]
            a[p, g + 8] = far[np.random.randint(len(far))]
    return np.exp2(a.ravel()).repeat(32)


def f64(x):
    return np.asarray(x).astype(np.float64)


def striped(idx):
    return np.tile(idx.reshape(-1, 16).T, (8, 1)).astype(np.uint16)


def unstriped(offs):
    return offs[:16].T.reshape(-1).astype(np.int64)


def striped8(idx):
    return np.concatenate([x.reshape(-1, 16).T for x in idx]).astype(np.uint16)


def runs(offs, k):
    lists = np.stack([offs[16 * r : 16 * r + 16].T.reshape(-1) for r in range(8)]).astype(np.int64)
    return lists[np.arange(k) % 512 // 64]


def pack_weight(w):
    k, n = w.shape
    w = f64(np.asarray(w, np.float32).astype(ml_dtypes.bfloat16)).reshape(k // 32, 32, n)
    amax = np.abs(w).max(1)
    byte = np.clip(np.where(amax > 0, np.frexp(amax)[1] - 1 + 127 - 7, 1), 1, 254)
    scaled = (w * np.exp2(127.0 - byte)[:, None, :]).reshape(k, n).astype(np.float32)
    words = np.ascontiguousarray(scaled.reshape(k // 512, 128, 4, n).transpose(0, 1, 3, 2)).astype(ml_dtypes.float8_e4m3fn).view(np.uint8)
    return words, np.ascontiguousarray(byte.astype(np.uint8).reshape(k // 512, 16, n))


def unpack_weight(words, scales):
    g, p, n, _ = words.shape
    vals = np.ascontiguousarray(words).view(ml_dtypes.float8_e4m3fn).astype(np.float64) * np.repeat(np.exp2(scales.astype(np.float64) - 127.0), 8, axis=1)[..., None]
    return vals.transpose(0, 1, 3, 2).reshape(g * 512, n)


def sigmoid(v):
    return 1.0 / (1.0 + np.exp(-np.maximum(v, -700.0)))

def planes(y):
    n, m = y.shape
    v = y.astype(np.float32).astype(ml_dtypes.bfloat16).astype(np.float64).reshape(n // 32, 32, m)
    top = np.abs(v).max(1)
    byte = np.clip(np.where(top > 0, np.frexp(top)[1] - 1 + 127 - 7, 1), 1, 254)
    codes = (v * np.exp2(127.0 - byte)[:, None, :]).reshape(n, m).astype(np.float32).astype(ml_dtypes.float8_e4m3fn).view(np.uint8)
    words = codes.reshape(n // 512, 128, 4, m).transpose(0, 1, 3, 2)
    return np.ascontiguousarray(words), np.ascontiguousarray(byte.astype(np.uint8).reshape(n // 512, 16, m))


K, T, S, N = 512, 2048, 512, 512


def setup_inputs():
    n = np.random.standard_normal
    s = mx_kscale(K)[:, None]
    packed_xT = pack_weight(n((K, T)) * s)
    return {
        "x_words": packed_xT[0],
        "x_scales": packed_xT[1],
        "w1": (n((K, N)) / np.sqrt(2 * K) / s).astype(np.float32),
        "w2": (n((K, N)) / np.sqrt(2 * K) / s).astype(np.float32),
        "w3": (n((K, N)) / np.sqrt(K) / s).astype(np.float32),
        "offs": striped8(np.random.randint(0, T, (8, S))),
        "own": striped(np.random.permutation(T)[:S]),
    }


def reference(x_words, x_scales, w1, w2, w3, offs, own):
    xq = unpack_weight(x_words, x_scales)[np.arange(K)[:, None], runs(offs, K)]
    x_own = unpack_weight(x_words, x_scales)[:, unstriped(own)]
    s = mxq(f64(w3), 0, "e4m3").T @ xq
    out_0 = ((mxq(f64(w1), 0, "e4m3").T @ xq + mxq(f64(w2), 0, "e4m3").T @ x_own)) * sigmoid(s)
    return (out_0,) + planes(out_0)

@@ -1,0 +1,159 @@
+from contextlib import ExitStack
+
+import concourse.mybir as mybir
+
+K, T, S, N = 512, 2048, 512, 512
+FLOPS = 3 * 2 * K * N * S
+
+F32 = mybir.dt.float32
+BF16 = mybir.dt.bfloat16
+I32 = mybir.dt.int32
+U32 = mybir.dt.uint32
+U16 = mybir.dt.uint16
+U8 = mybir.dt.uint8
+FP8X4 = mybir.dt.float8_e4m3fn_x4
+SIGMOID = mybir.ActivationFunctionType.Sigmoid
+MULT = mybir.AluOpType.mult
+
+P = 128
+PACK = 4
+QUADRANT = 32
+BLOCK_PARTITIONS = 8
+HALF = S // 2
+
+
+def tile_picked_ngramgate_none_po_kernel(
+    tc, x_words, x_scales, w1, w2, w3, offs, own, out_0, out_1, out_2
+):
+    nc = tc.nc
+    with ExitStack() as ctx:
+        keep = ctx.enter_context(tc.tile_pool(name="keep", bufs=1))
+        psum = ctx.enter_context(tc.psum_pool(name="psum", bufs=1))
+
+        offs_sb = keep.tile([P, S // 16], U16, name="offs_sb")
+        own_sb = keep.tile([P, S // 16], U16, name="own_sb")
+        nc.sync.dma_start(offs_sb[:], offs)
+        nc.sync.dma_start(own_sb[:], own)
+
+        scale_table = keep.tile([P, T], U8, name="scale_table", align_bytes=64)
+        nc.vector.memset(scale_table[:].bitcast(I32), 0)
+        nc.scalar.dma_start(scale_table[:].bitcast(I32)[0:P:BLOCK_PARTITIONS, :], x_scales[0].bitcast(I32))
+        x_planes = keep.tile([P, 2 * S], U8, name="x_planes", align_bytes=64)
+        nc.vector.memset(x_planes[:].bitcast(I32), 0)
+
+        def load_weight(w, name):
+            raw = keep.tile([P, PACK, N], F32, name=name + "_raw")
+            nc.sync.dma_start(raw[:], w.rearrange("(p j) c -> p j c", j=PACK))
+            return raw
+
+        w3_raw = load_weight(w3, "w3")
+        word_table = keep.tile([P, T], I32, name="word_table", align_bytes=64)
+        nc.sync.dma_start(word_table[:], x_words[0].rearrange("p c r -> p (c r)").bitcast(I32))
+        w1_raw = load_weight(w1, "w1")
+        w2_raw = load_weight(w2, "w2")
+
+        picked_scales = keep.tile([P, 2 * S], U8, name="picked_scales", align_bytes=64)
+        nc.vector.tensor_copy(picked_scales[:, 0:S], scale_table[:].indirect(offs_sb[:]))
+        nc.vector.tensor_copy(picked_scales[:, S : 2 * S], scale_table[:].indirect(own_sb[:]))
+        for b in range(PACK):
+            nc.scalar.dma_start(
+                x_planes[:].bitcast(I32)[b:P:QUADRANT, :],
+                picked_scales[:].bitcast(I32)[b * BLOCK_PARTITIONS : P : QUADRANT, :],
+            )
+
+        def round_weight(raw, name, vector_share):
+            dealt = keep.tile([P, PACK, P, PACK], BF16, name=name + "_bf16", align_bytes=64)
+            dst = dealt[:].rearrange("p t m j -> p m j t")
+            src = raw[:].rearrange("p j (m t) -> p m j t", t=PACK)
+            if vector_share < P:
+                nc.scalar.copy(dst[:, vector_share:P], src[:, vector_share:P])
+            nc.vector.tensor_copy(dst[:, 0:vector_share], src[:, 0:vector_share])
+            return dealt
+
+        def quantize_weight(dealt, name, pieces):
+            codes = keep.tile([P, N], U32, name=name + "_codes", align_bytes=64)
+            scales = keep.tile([P, N], U8, name=name + "_scales", align_bytes=64)
+            flat = dealt[:].rearrange("p t m j -> p (t m j)")
+            width = N // pieces
+            for c0 in range(0, N, width):
+                nc.vector.quantize_mx(
+                    out=codes[:, c0 : c0 + width].bitcast(FP8X4),
+                    scales=scales[:, c0 : c0 + width],
+                    in_=flat[:, PACK * c0 : PACK * (c0 + width)],
+                )
+            return codes, scales
+
+        def product(acc, weight, t, words, plane0, c0, width, start, stop):
+            codes, scales = weight
+            nc.tensor.matmul_mx(
+                out=acc,
+                lhsT=codes[:, t * P : (t + 1) * P].bitcast(FP8X4),
+                lhsT_scale=scales[:, t * P : (t + 1) * P],
+                rhs=words[:, c0 : c0 + width].bitcast(FP8X4),
+                rhs_scale=x_planes[:, plane0 + c0 : plane0 + c0 + width],
+                start=start,
+                stop=stop,
+            )
+
+        w3_mx = quantize_weight(round_weight(w3_raw, "w3", 64), "w3", 1)
+
+        hashed_words = keep.tile([P, S], U32, name="hashed_words", align_bytes=64)
+        own_words = keep.tile([P, S], U32, name="own_words", align_bytes=64)
+        nc.vector.tensor_copy(hashed_words[:], word_table[:].bitcast(U32).indirect(offs_sb[:]))
+        nc.vector.tensor_copy(own_words[:], word_table[:].bitcast(U32).indirect(own_sb[:]))
+
+        gates = []
+        for t in range(PACK):
+            logits = psum.tile([P, S], F32, name="logits", tag="bank%d" % (PACK + t))
+            product(logits[:], w3_mx, t, hashed_words, 0, 0, S, True, True)
+            gate = keep.tile([P, S], F32, name="gate%d" % t)
+            nc.scalar.activation(gate[:], logits[:], SIGMOID)
+            gates.append(gate)
+
+        w1_mx = quantize_weight(round_weight(w1_raw, "w1", P), "w1", 1)
+        sums = {}
+        for h in range(2):
+            for t in range(PACK):
+                sums[h, t] = psum.tile([P, S], F32, name="sums", tag="bank%d" % (PACK * h + t))
+                product(sums[h, t][:, 0:HALF], w1_mx, t, hashed_words, 0, h * HALF, HALF, True, False)
+
+        w2_mx = quantize_weight(round_weight(w2_raw, "w2", 84), "w2", 2)
+        for h in range(2):
+            for t in range(PACK):
+                product(sums[h, t][:, 0:HALF], w2_mx, t, own_words, S, h * HALF, HALF, False, True)
+
+        out_rows = out_0.rearrange("(p t) j -> p t j", t=PACK)
+        out_words = out_1[0].rearrange("p c r -> p (c r)").bitcast(I32)
+        y_scales = keep.tile([P, S], U8, name="y_scales", align_bytes=64)
+        y = []
+        for h in range(2):
+            cols = slice(h * HALF, (h + 1) * HALF)
+            y_half = keep.tile([P, PACK, HALF], F32, name="y%d" % h)
+            for t in range(PACK):
+                nc.vector.tensor_tensor(y_half[:, t, :], sums[h, t][:, 0:HALF], gates[t][:, cols], MULT)
+            nc.sync.dma_start(out_rows[:, :, cols], y_half[:])
+            y.append(y_half)
+
+        for h in range(2):
+            cols = slice(h * HALF, (h + 1) * HALF)
+            y_bf16 = keep.tile([P, HALF, PACK], BF16, name="y%d_bf16" % h, align_bytes=64)
+            dst = y_bf16[:].rearrange("p (c i) t -> p c t i", i=PACK)
+            src = y[h][:].rearrange("p t (c i) -> p c t i", i=PACK)
+            split = 0 if h == 0 else HALF // PACK // 2
+            nc.scalar.copy(dst[:, split:], src[:, split:])
+            if split:
+                nc.vector.tensor_copy(dst[:, 0:split], src[:, 0:split])
+            y_words = keep.tile([P, HALF], U32, name="y%d_words" % h, align_bytes=64)
+            nc.vector.quantize_mx(
+                out=y_words[:].bitcast(FP8X4),
+                scales=y_scales[:, cols],
+                in_=y_bf16[:].rearrange("p c t -> p (c t)"),
+            )
+            nc.sync.dma_start(out_words[:, cols], y_words[:].bitcast(I32))
+
+        for q in range(P // QUADRANT):
+            queue = nc.scalar if q % 2 == 0 else nc.sync
+            queue.dma_start(
+                out_2[0, PACK * q : PACK * (q + 1), :].bitcast(I32),
+                y_scales[:].bitcast(I32)[QUADRANT * q : QUADRANT * q + PACK, :],
+            )

@@ -30,6 +30,15 @@ def tile_picked_ngramgate_none_po_kernel(
         keep = ctx.enter_context(tc.tile_pool(name="keep", bufs=1))
         psum = ctx.enter_context(tc.psum_pool(name="psum", bufs=1))
 
+        w3_raw = keep.tile([P, PACK, N], F32, name="w3_raw")
+        w3_rows = w3.rearrange("(p j) c -> p j c", j=PACK)
+        nc.sync.dma_start(w3_raw[:, 0:1, :], w3_rows[:, 0:1, :])
+
+        warm_in = keep.tile([P, 1], F32, name="warm_in")
+        warm_out = keep.tile([P, 1], F32, name="warm_out")
+        nc.gpsimd.memset(warm_in[:], 0.0)
+        nc.scalar.activation(warm_out[:], warm_in[:], SIGMOID)
+
         offs_sb = keep.tile([P, S // 16], U16, name="offs_sb")
         own_sb = keep.tile([P, S // 16], U16, name="own_sb")
         nc.sync.dma_start(offs_sb[:], offs)
@@ -37,7 +46,7 @@ def tile_picked_ngramgate_none_po_kernel(
 
         scale_table = keep.tile([P, T], U8, name="scale_table", align_bytes=64)
         nc.vector.memset(scale_table[:].bitcast(I32), 0)
-        nc.scalar.dma_start(scale_table[:].bitcast(I32)[0:P:BLOCK_PARTITIONS, :], x_scales[0].bitcast(I32))
+        nc.sync.dma_start(scale_table[:].bitcast(I32)[0:P:BLOCK_PARTITIONS, :], x_scales[0].bitcast(I32))
         x_planes = keep.tile([P, 2 * S], U8, name="x_planes", align_bytes=64)
         nc.vector.memset(x_planes[:].bitcast(I32), 0)
 
@@ -46,40 +55,42 @@ def tile_picked_ngramgate_none_po_kernel(
             nc.sync.dma_start(raw[:], w.rearrange("(p j) c -> p j c", j=PACK))
             return raw
 
-        w3_raw = load_weight(w3, "w3")
+        nc.sync.dma_start(w3_raw[:, 1:PACK, :], w3_rows[:, 1:PACK, :])
         word_table = keep.tile([P, T], I32, name="word_table", align_bytes=64)
         nc.sync.dma_start(word_table[:], x_words[0].rearrange("p c r -> p (c r)").bitcast(I32))
-        w1_raw = load_weight(w1, "w1")
-        w2_raw = load_weight(w2, "w2")
+        w1_raw = keep.tile([P, PACK, N], F32, name="w1_raw")
+        w1_rows = w1.rearrange("(p j) c -> p j c", j=PACK)
+        nc.sync.dma_start(w1_raw[:, 0:3, :], w1_rows[:, 0:3, :])
 
         picked_scales = keep.tile([P, 2 * S], U8, name="picked_scales", align_bytes=64)
         nc.vector.tensor_copy(picked_scales[:, 0:S], scale_table[:].indirect(offs_sb[:]))
         nc.vector.tensor_copy(picked_scales[:, S : 2 * S], scale_table[:].indirect(own_sb[:]))
         for b in range(PACK):
-            nc.scalar.dma_start(
+            nc.sync.dma_start(
                 x_planes[:].bitcast(I32)[b:P:QUADRANT, :],
                 picked_scales[:].bitcast(I32)[b * BLOCK_PARTITIONS : P : QUADRANT, :],
             )
 
-        def round_weight(raw, name, vector_share):
-            dealt = keep.tile([P, PACK, P, PACK], BF16, name=name + "_bf16", align_bytes=64)
-            dst = dealt[:].rearrange("p t m j -> p m j t")
-            src = raw[:].rearrange("p j (m t) -> p m j t", t=PACK)
-            if vector_share < P:
-                nc.scalar.copy(dst[:, vector_share:P], src[:, vector_share:P])
-            nc.vector.tensor_copy(dst[:, 0:vector_share], src[:, 0:vector_share])
-            return dealt
+        nc.sync.dma_start(w1_raw[:, 3:PACK, :], w1_rows[:, 3:PACK, :])
+        w2_raw = load_weight(w2, "w2")
 
-        def quantize_weight(dealt, name, pieces):
+        def quantize_weight(raw, name, vector_share, order):
+            src = raw[:].rearrange("p j (m t) -> p m j t", t=PACK)
+            pairs = [keep.tile([P, 2, P, PACK], BF16, name=name + "_bf16_%d" % u, align_bytes=64) for u in range(2)]
+            dst = [pair[:].rearrange("p t m j -> p m j t") for pair in pairs]
+            if vector_share < P:
+                nc.scalar.copy(dst[1][:, vector_share:P], src[:, vector_share:P, :, 2:4])
+            nc.vector.tensor_copy(dst[0], src[:, :, :, 0:2])
+            if vector_share > 0:
+                nc.vector.tensor_copy(dst[1][:, 0:vector_share], src[:, 0:vector_share, :, 2:4])
             codes = keep.tile([P, N], U32, name=name + "_codes", align_bytes=64)
             scales = keep.tile([P, N], U8, name=name + "_scales", align_bytes=64)
-            flat = dealt[:].rearrange("p t m j -> p (t m j)")
-            width = N // pieces
-            for c0 in range(0, N, width):
+            for u in order:
+                cols = slice(u * 2 * P, (u + 1) * 2 * P)
                 nc.vector.quantize_mx(
-                    out=codes[:, c0 : c0 + width].bitcast(FP8X4),
-                    scales=scales[:, c0 : c0 + width],
-                    in_=flat[:, PACK * c0 : PACK * (c0 + width)],
+                    out=codes[:, cols].bitcast(FP8X4),
+                    scales=scales[:, cols],
+                    in_=pairs[u][:].rearrange("p t m j -> p (t m j)"),
                 )
             return codes, scales
 
@@ -95,7 +106,7 @@ def tile_picked_ngramgate_none_po_kernel(
                 stop=stop,
             )
 
-        w3_mx = quantize_weight(round_weight(w3_raw, "w3", 64), "w3", 1)
+        w3_mx = quantize_weight(w3_raw, "w3", 0, (1, 0))
 
         hashed_words = keep.tile([P, S], U32, name="hashed_words", align_bytes=64)
         own_words = keep.tile([P, S], U32, name="own_words", align_bytes=64)
@@ -110,14 +121,14 @@ def tile_picked_ngramgate_none_po_kernel(
             nc.scalar.activation(gate[:], logits[:], SIGMOID)
             gates.append(gate)
 
-        w1_mx = quantize_weight(round_weight(w1_raw, "w1", P), "w1", 1)
+        w1_mx = quantize_weight(w1_raw, "w1", P, (0, 1))
         sums = {}
         for h in range(2):
             for t in range(PACK):
                 sums[h, t] = psum.tile([P, S], F32, name="sums", tag="bank%d" % (PACK * h + t))
                 product(sums[h, t][:, 0:HALF], w1_mx, t, hashed_words, 0, h * HALF, HALF, True, False)
 
-        w2_mx = quantize_weight(round_weight(w2_raw, "w2", 84), "w2", 2)
+        w2_mx = quantize_weight(w2_raw, "w2", 48, (0, 1))
         for h in range(2):
             for t in range(PACK):
                 product(sums[h, t][:, 0:HALF], w2_mx, t, own_words, S, h * HALF, HALF, False, True)
@@ -125,31 +136,41 @@ def tile_picked_ngramgate_none_po_kernel(
         out_rows = out_0.rearrange("(p t) j -> p t j", t=PACK)
         out_words = out_1[0].rearrange("p c r -> p (c r)").bitcast(I32)
         y_scales = keep.tile([P, S], U8, name="y_scales", align_bytes=64)
-        y = []
-        for h in range(2):
-            cols = slice(h * HALF, (h + 1) * HALF)
-            y_half = keep.tile([P, PACK, HALF], F32, name="y%d" % h)
-            for t in range(PACK):
-                nc.vector.tensor_tensor(y_half[:, t, :], sums[h, t][:, 0:HALF], gates[t][:, cols], MULT)
-            nc.sync.dma_start(out_rows[:, :, cols], y_half[:])
-            y.append(y_half)
+        y = [keep.tile([P, PACK, HALF], F32, name="y%d" % h) for h in range(2)]
+        y_bf16 = [keep.tile([P, HALF, PACK], BF16, name="y%d_bf16" % h, align_bytes=64) for h in range(2)]
 
-        for h in range(2):
+        def gate_sums(h, c0, c1):
+            for t in range(PACK):
+                nc.vector.tensor_tensor(
+                    y[h][:, t, c0:c1], sums[h, t][:, c0:c1], gates[t][:, h * HALF + c0 : h * HALF + c1], MULT
+                )
+
+        def round_y(copy, h, c0, c1):
+            copy(
+                y_bf16[h][:, c0:c1, :].rearrange("p (c i) t -> p c t i", i=PACK),
+                y[h][:, :, c0:c1].rearrange("p t (c i) -> p c t i", i=PACK),
+            )
+
+        def quantize_y(h):
             cols = slice(h * HALF, (h + 1) * HALF)
-            y_bf16 = keep.tile([P, HALF, PACK], BF16, name="y%d_bf16" % h, align_bytes=64)
-            dst = y_bf16[:].rearrange("p (c i) t -> p c t i", i=PACK)
-            src = y[h][:].rearrange("p t (c i) -> p c t i", i=PACK)
-            split = 0 if h == 0 else HALF // PACK // 2
-            nc.scalar.copy(dst[:, split:], src[:, split:])
-            if split:
-                nc.vector.tensor_copy(dst[:, 0:split], src[:, 0:split])
             y_words = keep.tile([P, HALF], U32, name="y%d_words" % h, align_bytes=64)
             nc.vector.quantize_mx(
                 out=y_words[:].bitcast(FP8X4),
                 scales=y_scales[:, cols],
-                in_=y_bf16[:].rearrange("p c t -> p (c t)"),
+                in_=y_bf16[h][:].rearrange("p c t -> p (c t)"),
             )
             nc.sync.dma_start(out_words[:, cols], y_words[:].bitcast(I32))
+
+        for c0 in (0, HALF // 2):
+            gate_sums(0, c0, c0 + HALF // 2)
+            round_y(nc.scalar.copy, 0, c0, c0 + HALF // 2)
+        nc.sync.dma_start(out_rows[:, :, 0:HALF], y[0][:])
+        gate_sums(1, 0, HALF)
+        nc.sync.dma_start(out_rows[:, :, HALF:S], y[1][:])
+        quantize_y(0)
+        round_y(nc.scalar.copy, 1, 160, HALF)
+        round_y(nc.vector.tensor_copy, 1, 0, 160)
+        quantize_y(1)
 
         for q in range(P // QUADRANT):
             queue = nc.scalar if q % 2 == 0 else nc.sync

@@ -34,21 +34,24 @@ def tile_picked_ngramgate_none_po_kernel(
         w3_rows = w3.rearrange("(p j) c -> p j c", j=PACK)
         nc.sync.dma_start(w3_raw[:, 0:1, :], w3_rows[:, 0:1, :])
 
-        warm_in = keep.tile([P, 1], F32, name="warm_in")
-        warm_out = keep.tile([P, 1], F32, name="warm_out")
-        nc.gpsimd.memset(warm_in[:], 0.0)
-        nc.scalar.activation(warm_out[:], warm_in[:], SIGMOID)
-
         offs_sb = keep.tile([P, S // 16], U16, name="offs_sb")
         own_sb = keep.tile([P, S // 16], U16, name="own_sb")
         nc.sync.dma_start(offs_sb[:], offs)
         nc.sync.dma_start(own_sb[:], own)
 
         scale_table = keep.tile([P, T], U8, name="scale_table", align_bytes=64)
-        nc.vector.memset(scale_table[:].bitcast(I32), 0)
+        nc.vector.memset(scale_table[:, 0 : T // 2].bitcast(I32), 0)
+        nc.gpsimd.memset(scale_table[:, T // 2 : T].bitcast(I32), 0)
         nc.sync.dma_start(scale_table[:].bitcast(I32)[0:P:BLOCK_PARTITIONS, :], x_scales[0].bitcast(I32))
-        x_planes = keep.tile([P, 2 * S], U8, name="x_planes", align_bytes=64)
-        nc.vector.memset(x_planes[:].bitcast(I32), 0)
+
+        warm_in = keep.tile([P, 1], F32, name="warm_in")
+        warm_out = keep.tile([P, 1], F32, name="warm_out")
+        nc.gpsimd.memset(warm_in[:], 0.0)
+        nc.scalar.activation(warm_out[:], warm_in[:], SIGMOID)
+
+        x_planes = [keep.tile([P, S], U8, name="x_plane%d" % u, align_bytes=64) for u in range(2)]
+        for plane in x_planes:
+            nc.vector.memset(plane[:].bitcast(I32), 0)
 
         def load_weight(w, name):
             raw = keep.tile([P, PACK, N], F32, name=name + "_raw")
@@ -58,55 +61,57 @@ def tile_picked_ngramgate_none_po_kernel(
         nc.sync.dma_start(w3_raw[:, 1:PACK, :], w3_rows[:, 1:PACK, :])
         word_table = keep.tile([P, T], I32, name="word_table", align_bytes=64)
         nc.sync.dma_start(word_table[:], x_words[0].rearrange("p c r -> p (c r)").bitcast(I32))
-        w1_raw = keep.tile([P, PACK, N], F32, name="w1_raw")
-        w1_rows = w1.rearrange("(p j) c -> p j c", j=PACK)
-        nc.sync.dma_start(w1_raw[:, 0:3, :], w1_rows[:, 0:3, :])
 
-        picked_scales = keep.tile([P, 2 * S], U8, name="picked_scales", align_bytes=64)
-        nc.vector.tensor_copy(picked_scales[:, 0:S], scale_table[:].indirect(offs_sb[:]))
-        nc.vector.tensor_copy(picked_scales[:, S : 2 * S], scale_table[:].indirect(own_sb[:]))
-        for b in range(PACK):
-            nc.sync.dma_start(
-                x_planes[:].bitcast(I32)[b:P:QUADRANT, :],
-                picked_scales[:].bitcast(I32)[b * BLOCK_PARTITIONS : P : QUADRANT, :],
-            )
+        picked_scales = [keep.tile([P, S], U8, name="picked_scales%d" % u, align_bytes=64) for u in range(2)]
+        nc.vector.tensor_copy(picked_scales[0][:], scale_table[:].indirect(offs_sb[:]))
+        nc.vector.tensor_copy(picked_scales[1][:], scale_table[:].indirect(own_sb[:]))
 
-        nc.sync.dma_start(w1_raw[:, 3:PACK, :], w1_rows[:, 3:PACK, :])
+        def place_scale_rows(u):
+            for b in range(PACK):
+                nc.sync.dma_start(
+                    x_planes[u][:].bitcast(I32)[b:P:QUADRANT, :],
+                    picked_scales[u][:].bitcast(I32)[b * BLOCK_PARTITIONS : P : QUADRANT, :],
+                )
+
+        place_scale_rows(0)
+        w1_raw = load_weight(w1, "w1")
         w2_raw = load_weight(w2, "w2")
+        place_scale_rows(1)
 
-        def quantize_weight(raw, name, vector_share, order):
+        def quantize_weight(raw, name, vector_shares, pieces):
             src = raw[:].rearrange("p j (m t) -> p m j t", t=PACK)
             pairs = [keep.tile([P, 2, P, PACK], BF16, name=name + "_bf16_%d" % u, align_bytes=64) for u in range(2)]
-            dst = [pair[:].rearrange("p t m j -> p m j t") for pair in pairs]
-            if vector_share < P:
-                nc.scalar.copy(dst[1][:, vector_share:P], src[:, vector_share:P, :, 2:4])
-            nc.vector.tensor_copy(dst[0], src[:, :, :, 0:2])
-            if vector_share > 0:
-                nc.vector.tensor_copy(dst[1][:, 0:vector_share], src[:, 0:vector_share, :, 2:4])
+            for u, share in enumerate(vector_shares):
+                dst = pairs[u][:].rearrange("p t m j -> p m j t")
+                if share < P:
+                    nc.scalar.copy(dst[:, share:P], src[:, share:P, :, 2 * u : 2 * u + 2])
+                if share > 0:
+                    nc.vector.tensor_copy(dst[:, 0:share], src[:, 0:share, :, 2 * u : 2 * u + 2])
             codes = keep.tile([P, N], U32, name=name + "_codes", align_bytes=64)
             scales = keep.tile([P, N], U8, name=name + "_scales", align_bytes=64)
-            for u in order:
-                cols = slice(u * 2 * P, (u + 1) * 2 * P)
+            for t0, t1 in pieces:
+                cols = slice(t0 * P, t1 * P)
+                u = t0 // 2
                 nc.vector.quantize_mx(
                     out=codes[:, cols].bitcast(FP8X4),
                     scales=scales[:, cols],
-                    in_=pairs[u][:].rearrange("p t m j -> p (t m j)"),
+                    in_=pairs[u][:, t0 - 2 * u : t1 - 2 * u].rearrange("p t m j -> p (t m j)"),
                 )
             return codes, scales
 
-        def product(acc, weight, t, words, plane0, c0, width, start, stop):
+        def product(acc, weight, t, words, plane, c0, width, start, stop):
             codes, scales = weight
             nc.tensor.matmul_mx(
                 out=acc,
                 lhsT=codes[:, t * P : (t + 1) * P].bitcast(FP8X4),
                 lhsT_scale=scales[:, t * P : (t + 1) * P],
                 rhs=words[:, c0 : c0 + width].bitcast(FP8X4),
-                rhs_scale=x_planes[:, plane0 + c0 : plane0 + c0 + width],
+                rhs_scale=plane[:, c0 : c0 + width],
                 start=start,
                 stop=stop,
             )
 
-        w3_mx = quantize_weight(w3_raw, "w3", 0, (1, 0))
+        w3_mx = quantize_weight(w3_raw, "w3", (0, P), ((0, 2), (2, 4)))
 
         hashed_words = keep.tile([P, S], U32, name="hashed_words", align_bytes=64)
         own_words = keep.tile([P, S], U32, name="own_words", align_bytes=64)
@@ -116,22 +121,21 @@ def tile_picked_ngramgate_none_po_kernel(
         gates = []
         for t in range(PACK):
             logits = psum.tile([P, S], F32, name="logits", tag="bank%d" % (PACK + t))
-            product(logits[:], w3_mx, t, hashed_words, 0, 0, S, True, True)
+            product(logits[:], w3_mx, t, hashed_words, x_planes[0], 0, S, True, True)
             gate = keep.tile([P, S], F32, name="gate%d" % t)
             nc.scalar.activation(gate[:], logits[:], SIGMOID)
             gates.append(gate)
 
-        w1_mx = quantize_weight(w1_raw, "w1", P, (0, 1))
+        w1_mx = quantize_weight(w1_raw, "w1", (P, P), ((0, 2), (2, 4)))
         sums = {}
         for h in range(2):
             for t in range(PACK):
                 sums[h, t] = psum.tile([P, S], F32, name="sums", tag="bank%d" % (PACK * h + t))
-                product(sums[h, t][:, 0:HALF], w1_mx, t, hashed_words, 0, h * HALF, HALF, True, False)
+                product(sums[h, t][:, 0:HALF], w1_mx, t, hashed_words, x_planes[0], h * HALF, HALF, True, False)
 
-        w2_mx = quantize_weight(w2_raw, "w2", 48, (0, 1))
-        for h in range(2):
-            for t in range(PACK):
-                product(sums[h, t][:, 0:HALF], w2_mx, t, own_words, S, h * HALF, HALF, False, True)
+        w2_mx = quantize_weight(w2_raw, "w2", (100, 72), ((0, 1), (1, 2), (2, 3), (3, 4)))
+        for h, t in ((0, 0), (1, 0), (0, 1), (1, 1), (0, 2), (0, 3), (1, 2), (1, 3)):
+            product(sums[h, t][:, 0:HALF], w2_mx, t, own_words, x_planes[1], h * HALF, HALF, False, True)
 
         out_rows = out_0.rearrange("(p t) j -> p t j", t=PACK)
         out_words = out_1[0].rearrange("p c r -> p (c r)").bitcast(I32)
@@ -139,8 +143,8 @@ def tile_picked_ngramgate_none_po_kernel(
         y = [keep.tile([P, PACK, HALF], F32, name="y%d" % h) for h in range(2)]
         y_bf16 = [keep.tile([P, HALF, PACK], BF16, name="y%d_bf16" % h, align_bytes=64) for h in range(2)]
 
-        def gate_sums(h, c0, c1):
-            for t in range(PACK):
+        def gate_sums(h, tiles, c0, c1):
+            for t in tiles:
                 nc.vector.tensor_tensor(
                     y[h][:, t, c0:c1], sums[h, t][:, c0:c1], gates[t][:, h * HALF + c0 : h * HALF + c1], MULT
                 )
@@ -151,26 +155,35 @@ def tile_picked_ngramgate_none_po_kernel(
                 y[h][:, :, c0:c1].rearrange("p t (c i) -> p c t i", i=PACK),
             )
 
-        def quantize_y(h):
-            cols = slice(h * HALF, (h + 1) * HALF)
-            y_words = keep.tile([P, HALF], U32, name="y%d_words" % h, align_bytes=64)
-            nc.vector.quantize_mx(
-                out=y_words[:].bitcast(FP8X4),
-                scales=y_scales[:, cols],
-                in_=y_bf16[h][:].rearrange("p c t -> p (c t)"),
-            )
-            nc.sync.dma_start(out_words[:, cols], y_words[:].bitcast(I32))
+        y_words = [keep.tile([P, HALF], U32, name="y%d_words" % h, align_bytes=64) for h in range(2)]
 
-        for c0 in (0, HALF // 2):
-            gate_sums(0, c0, c0 + HALF // 2)
-            round_y(nc.scalar.copy, 0, c0, c0 + HALF // 2)
-        nc.sync.dma_start(out_rows[:, :, 0:HALF], y[0][:])
-        gate_sums(1, 0, HALF)
+        def quantize_y(h, c0, c1):
+            nc.vector.quantize_mx(
+                out=y_words[h][:, c0:c1].bitcast(FP8X4),
+                scales=y_scales[:, h * HALF + c0 : h * HALF + c1],
+                in_=y_bf16[h][:, c0:c1, :].rearrange("p c t -> p (c t)"),
+            )
+
+        quarter = HALF // 2
+        for t in (0, 1):
+            staged = keep.tile([P, HALF], F32, name="staged%d" % t)
+            nc.scalar.copy(staged[:], sums[1, t][:, 0:HALF])
+            nc.gpsimd.tensor_tensor(y[1][:, t, :], staged[:], gates[t][:, HALF:S], MULT)
+        gate_sums(0, (0, 1), 0, HALF)
+        nc.sync.dma_start(out_rows[:, 0:2, 0:HALF], y[0][:, 0:2, :])
+        for c0 in (0, quarter):
+            gate_sums(0, (2, 3), c0, c0 + quarter)
+            round_y(nc.scalar.copy, 0, c0, c0 + quarter)
+        nc.sync.dma_start(out_rows[:, 2:PACK, 0:HALF], y[0][:, 2:PACK, :])
+        gate_sums(1, (2, 3), 0, HALF)
         nc.sync.dma_start(out_rows[:, :, HALF:S], y[1][:])
-        quantize_y(0)
+        quantize_y(0, 0, quarter)
         round_y(nc.scalar.copy, 1, 160, HALF)
         round_y(nc.vector.tensor_copy, 1, 0, 160)
-        quantize_y(1)
+        quantize_y(0, quarter, HALF)
+        nc.sync.dma_start(out_words[:, 0:HALF], y_words[0][:].bitcast(I32))
+        quantize_y(1, 0, HALF)
+        nc.sync.dma_start(out_words[:, HALF:S], y_words[1][:].bitcast(I32))
 
         for q in range(P // QUADRANT):
             queue = nc.scalar if q % 2 == 0 else nc.sync

@@ -134,13 +134,20 @@ def tile_picked_ngramgate_none_po_kernel(
                 product(sums[h, t][:, 0:HALF], w1_mx, t, hashed_words, x_planes[0], h * HALF, HALF, True, False)
 
         w2_mx = quantize_weight(w2_raw, "w2", (100, 72), ((0, 1), (1, 2), (2, 3), (3, 4)))
-        for h, t in ((0, 0), (1, 0), (0, 1), (1, 1), (0, 2), (0, 3), (1, 2), (1, 3)):
+        for h, t in ((0, 0), (1, 0), (0, 1), (1, 1), (0, 2), (0, 3), (1, 3), (1, 2)):
             product(sums[h, t][:, 0:HALF], w2_mx, t, own_words, x_planes[1], h * HALF, HALF, False, True)
 
-        out_rows = out_0.rearrange("(p t) j -> p t j", t=PACK)
+        out_run = out_0.rearrange("(p t) j -> p (t j)", t=PACK)
         out_words = out_1[0].rearrange("p c r -> p (c r)").bitcast(I32)
         y_scales = keep.tile([P, S], U8, name="y_scales", align_bytes=64)
-        y = [keep.tile([P, PACK, HALF], F32, name="y%d" % h) for h in range(2)]
+        y_all = keep.tile([P, PACK * S], F32, name="y")
+        y_rows = y_all[:].rearrange("p (t j) -> p t j", t=PACK)
+        y = [y_rows[:, :, h * HALF : (h + 1) * HALF] for h in range(2)]
+
+        def store_y(first, last):
+            run = slice(first * HALF, last * HALF)
+            nc.sync.dma_start(out_run[:, run], y_all[:, run])
+
         y_bf16 = [keep.tile([P, HALF, PACK], BF16, name="y%d_bf16" % h, align_bytes=64) for h in range(2)]
 
         def gate_sums(h, tiles, c0, c1):
@@ -169,14 +176,23 @@ def tile_picked_ngramgate_none_po_kernel(
             staged = keep.tile([P, HALF], F32, name="staged%d" % t)
             nc.scalar.copy(staged[:], sums[1, t][:, 0:HALF])
             nc.gpsimd.tensor_tensor(y[1][:, t, :], staged[:], gates[t][:, HALF:S], MULT)
-        gate_sums(0, (0, 1), 0, HALF)
-        nc.sync.dma_start(out_rows[:, 0:2, 0:HALF], y[0][:, 0:2, :])
-        for c0 in (0, quarter):
-            gate_sums(0, (2, 3), c0, c0 + quarter)
-            round_y(nc.scalar.copy, 0, c0, c0 + quarter)
-        nc.sync.dma_start(out_rows[:, 2:PACK, 0:HALF], y[0][:, 2:PACK, :])
-        gate_sums(1, (2, 3), 0, HALF)
-        nc.sync.dma_start(out_rows[:, :, HALF:S], y[1][:])
+        gate_sums(0, (0,), 0, HALF)
+        store_y(0, 1)
+        gate_sums(0, (1,), 0, HALF)
+        store_y(2, 3)
+        gate_sums(0, (2, 3), 0, quarter)
+        round_y(nc.scalar.copy, 0, 0, quarter)
+        gate_sums(0, (3,), quarter, HALF)
+        store_y(6, 7)
+        gate_sums(0, (2,), quarter, HALF)
+        round_y(nc.scalar.copy, 0, quarter, HALF)
+        gate_sums(1, (3,), 0, HALF)
+        nc.sync.dma_start(
+            out_run.rearrange("p (a j) -> p a j", j=HALF)[:, 1:8:6, :],
+            y_all[:].rearrange("p (a j) -> p a j", j=HALF)[:, 1:8:6, :],
+        )
+        gate_sums(1, (2,), 0, HALF)
+        store_y(3, 6)
         quantize_y(0, 0, quarter)
         round_y(nc.scalar.copy, 1, 160, HALF)
         round_y(nc.vector.tensor_copy, 1, 0, 160)

@@ -111,7 +111,7 @@ def tile_picked_ngramgate_none_po_kernel(
                 stop=stop,
             )
 
-        w3_mx = quantize_weight(w3_raw, "w3", (0, P), ((0, 2), (2, 4)))
+        w3_mx = quantize_weight(w3_raw, "w3", (0, 88), ((0, 2), (2, 4)))
 
         hashed_words = keep.tile([P, S], U32, name="hashed_words", align_bytes=64)
         own_words = keep.tile([P, S], U32, name="own_words", align_bytes=64)
@@ -133,7 +133,34 @@ def tile_picked_ngramgate_none_po_kernel(
                 sums[h, t] = psum.tile([P, S], F32, name="sums", tag="bank%d" % (PACK * h + t))
                 product(sums[h, t][:, 0:HALF], w1_mx, t, hashed_words, x_planes[0], h * HALF, HALF, True, False)
 
-        w2_mx = quantize_weight(w2_raw, "w2", (100, 72), ((0, 1), (1, 2), (2, 3), (3, 4)))
+        w2_src = w2_raw[:].rearrange("p j (m t) -> p m j t", t=PACK)
+        w2_pairs = [keep.tile([P, 2, P, PACK], BF16, name="w2_bf16_%d" % u, align_bytes=64) for u in range(2)]
+        w2_mx = (
+            keep.tile([P, N], U32, name="w2_codes", align_bytes=64),
+            keep.tile([P, N], U8, name="w2_scales", align_bytes=64),
+        )
+
+        def round_w2(copy, u, m0, m1):
+            dst = w2_pairs[u][:].rearrange("p t m j -> p m j t")
+            copy(dst[:, m0:m1], w2_src[:, m0:m1, :, 2 * u : 2 * u + 2])
+
+        def quantize_w2(t):
+            cols = slice(t * P, (t + 1) * P)
+            nc.vector.quantize_mx(
+                out=w2_mx[0][:, cols].bitcast(FP8X4),
+                scales=w2_mx[1][:, cols],
+                in_=w2_pairs[t // 2][:, t % 2].rearrange("p m j -> p (m j)"),
+            )
+
+        round_w2(nc.vector.tensor_copy, 0, 0, 84)
+        round_w2(nc.scalar.copy, 0, 84, P)
+        round_w2(nc.vector.tensor_copy, 1, 0, 44)
+        round_w2(nc.scalar.copy, 1, 88, P)
+        quantize_w2(0)
+        quantize_w2(1)
+        round_w2(nc.vector.tensor_copy, 1, 44, 88)
+        quantize_w2(2)
+        quantize_w2(3)
         for h, t in ((0, 0), (1, 0), (0, 1), (1, 1), (0, 2), (0, 3), (1, 3), (1, 2)):
             product(sums[h, t][:, 0:HALF], w2_mx, t, own_words, x_planes[1], h * HALF, HALF, False, True)
 

@@ -54,7 +54,7 @@ def tile_picked_ngramgate_none_po_kernel(
             nc.vector.memset(plane[:].bitcast(I32), 0)
 
         def load_weight(w, name):
-            raw = keep.tile([P, PACK, N], F32, name=name + "_raw")
+            raw = keep.tile([P, PACK, N], F32, name=name + "_raw", tag=name + "_raw")
             nc.sync.dma_start(raw[:], w.rearrange("(p j) c -> p j c", j=PACK))
             return raw
 
@@ -118,20 +118,31 @@ def tile_picked_ngramgate_none_po_kernel(
         nc.vector.tensor_copy(hashed_words[:], word_table[:].bitcast(U32).indirect(offs_sb[:]))
         nc.vector.tensor_copy(own_words[:], word_table[:].bitcast(U32).indirect(own_sb[:]))
 
-        gates = []
+        gates = {}
+        logits = []
+
+        def make_gate(t, h0, h1, tag):
+            gate = keep.tile([P, (h1 - h0) * HALF], F32, name="gate%d_%d" % (t, h0), tag=tag)
+            nc.scalar.activation(gate[:], logits[t][:, h0 * HALF : h1 * HALF], SIGMOID)
+            for h in range(h0, h1):
+                gates[h, t] = gate[:, (h - h0) * HALF : (h - h0 + 1) * HALF]
+
         for t in range(PACK):
-            logits = psum.tile([P, S], F32, name="logits", tag="bank%d" % (PACK + t))
-            product(logits[:], w3_mx, t, hashed_words, x_planes[0], 0, S, True, True)
-            gate = keep.tile([P, S], F32, name="gate%d" % t)
-            nc.scalar.activation(gate[:], logits[:], SIGMOID)
-            gates.append(gate)
+            logits.append(psum.tile([P, S], F32, name="logits", tag="bank%d" % (PACK + t)))
+            product(logits[t][:], w3_mx, t, hashed_words, x_planes[0], 0, S, True, True)
+            make_gate(t, 0, 2 if t < PACK - 1 else 1, "gate%d" % t)
 
         w1_mx = quantize_weight(w1_raw, "w1", (P, P), ((0, 2), (2, 4)))
         sums = {}
         for h in range(2):
-            for t in range(PACK):
-                sums[h, t] = psum.tile([P, S], F32, name="sums", tag="bank%d" % (PACK * h + t))
-                product(sums[h, t][:, 0:HALF], w1_mx, t, hashed_words, x_planes[0], h * HALF, HALF, True, False)
+            for t in range(PACK - 1):
+                bank = psum.tile([P, S], F32, name="sums", tag="bank%d" % (PACK * h + t))
+                sums[h, t] = bank[:, 0:HALF]
+                product(sums[h, t], w1_mx, t, hashed_words, x_planes[0], h * HALF, HALF, True, False)
+        last_sums = psum.tile([P, S], F32, name="sums", tag="bank3")
+        product(last_sums[:], w1_mx, 3, hashed_words, x_planes[0], 0, S, True, False)
+        sums[0, 3] = last_sums[:, 0:HALF]
+        sums[1, 3] = last_sums[:, HALF:S]
 
         w2_src = w2_raw[:].rearrange("p j (m t) -> p m j t", t=PACK)
         w2_pairs = [keep.tile([P, 2, P, PACK], BF16, name="w2_bf16_%d" % u, align_bytes=64) for u in range(2)]
@@ -154,15 +165,17 @@ def tile_picked_ngramgate_none_po_kernel(
 
         round_w2(nc.vector.tensor_copy, 0, 0, 84)
         round_w2(nc.scalar.copy, 0, 84, P)
-        round_w2(nc.vector.tensor_copy, 1, 0, 44)
-        round_w2(nc.scalar.copy, 1, 88, P)
+        round_w2(nc.vector.tensor_copy, 1, 0, 36)
+        round_w2(nc.scalar.copy, 1, 72, P)
         quantize_w2(0)
         quantize_w2(1)
-        round_w2(nc.vector.tensor_copy, 1, 44, 88)
+        round_w2(nc.vector.tensor_copy, 1, 36, 72)
         quantize_w2(2)
         quantize_w2(3)
-        for h, t in ((0, 0), (1, 0), (0, 1), (1, 1), (0, 2), (0, 3), (1, 3), (1, 2)):
-            product(sums[h, t][:, 0:HALF], w2_mx, t, own_words, x_planes[1], h * HALF, HALF, False, True)
+        make_gate(PACK - 1, 1, 2, "w2_raw")
+        for h, t in ((0, 0), (1, 1), (1, 0), (0, 1), (0, 2), (1, 2)):
+            product(sums[h, t], w2_mx, t, own_words, x_planes[1], h * HALF, HALF, False, True)
+        product(last_sums[:], w2_mx, 3, own_words, x_planes[1], 0, S, False, True)
 
         out_run = out_0.rearrange("(p t) j -> p (t j)", t=PACK)
         out_words = out_1[0].rearrange("p c r -> p (c r)").bitcast(I32)
@@ -180,7 +193,7 @@ def tile_picked_ngramgate_none_po_kernel(
         def gate_sums(h, tiles, c0, c1):
             for t in tiles:
                 nc.vector.tensor_tensor(
-                    y[h][:, t, c0:c1], sums[h, t][:, c0:c1], gates[t][:, h * HALF + c0 : h * HALF + c1], MULT
+                    y[h][:, t, c0:c1], sums[h, t][:, c0:c1], gates[h, t][:, c0:c1], MULT
                 )
 
         def round_y(copy, h, c0, c1):
@@ -199,30 +212,27 @@ def tile_picked_ngramgate_none_po_kernel(
             )
 
         quarter = HALF // 2
-        for t in (0, 1):
+        for t in (1, 2):
             staged = keep.tile([P, HALF], F32, name="staged%d" % t)
-            nc.scalar.copy(staged[:], sums[1, t][:, 0:HALF])
-            nc.gpsimd.tensor_tensor(y[1][:, t, :], staged[:], gates[t][:, HALF:S], MULT)
+            nc.scalar.copy(staged[:], sums[1, t])
+            nc.gpsimd.tensor_tensor(y[1][:, t, :], staged[:], gates[1, t], MULT)
         gate_sums(0, (0,), 0, HALF)
         store_y(0, 1)
+        gate_sums(1, (0,), 0, HALF)
+        store_y(1, 2)
         gate_sums(0, (1,), 0, HALF)
         store_y(2, 3)
         gate_sums(0, (2, 3), 0, quarter)
         round_y(nc.scalar.copy, 0, 0, quarter)
-        gate_sums(0, (3,), quarter, HALF)
-        store_y(6, 7)
         gate_sums(0, (2,), quarter, HALF)
+        store_y(3, 5)
+        gate_sums(0, (3,), quarter, HALF)
         round_y(nc.scalar.copy, 0, quarter, HALF)
         gate_sums(1, (3,), 0, HALF)
-        nc.sync.dma_start(
-            out_run.rearrange("p (a j) -> p a j", j=HALF)[:, 1:8:6, :],
-            y_all[:].rearrange("p (a j) -> p a j", j=HALF)[:, 1:8:6, :],
-        )
-        gate_sums(1, (2,), 0, HALF)
-        store_y(3, 6)
+        store_y(5, 8)
         quantize_y(0, 0, quarter)
-        round_y(nc.scalar.copy, 1, 160, HALF)
-        round_y(nc.vector.tensor_copy, 1, 0, 160)
+        round_y(nc.scalar.copy, 1, 192, HALF)
+        round_y(nc.vector.tensor_copy, 1, 0, 192)
         quantize_y(0, quarter, HALF)
         nc.sync.dma_start(out_words[:, 0:HALF], y_words[0][:].bitcast(I32))
         quantize_y(1, 0, HALF)

@@ -20,6 +20,7 @@ PACK = 4
 QUADRANT = 32
 BLOCK_PARTITIONS = 8
 HALF = S // 2
+DMA_ALIGN = 256
 
 
 def tile_picked_ngramgate_none_po_kernel(
@@ -30,16 +31,16 @@ def tile_picked_ngramgate_none_po_kernel(
         keep = ctx.enter_context(tc.tile_pool(name="keep", bufs=1))
         psum = ctx.enter_context(tc.psum_pool(name="psum", bufs=1))
 
-        w3_raw = keep.tile([P, PACK, N], F32, name="w3_raw")
+        w3_raw = keep.tile([P, PACK, N], F32, name="w3_raw", align_bytes=DMA_ALIGN)
         w3_rows = w3.rearrange("(p j) c -> p j c", j=PACK)
         nc.sync.dma_start(w3_raw[:, 0:1, :], w3_rows[:, 0:1, :])
 
-        offs_sb = keep.tile([P, S // 16], U16, name="offs_sb")
-        own_sb = keep.tile([P, S // 16], U16, name="own_sb")
+        offs_sb = keep.tile([P, S // 16], U16, name="offs_sb", align_bytes=DMA_ALIGN)
+        own_sb = keep.tile([P, S // 16], U16, name="own_sb", align_bytes=DMA_ALIGN)
         nc.sync.dma_start(offs_sb[:], offs)
         nc.sync.dma_start(own_sb[:], own)
 
-        scale_table = keep.tile([P, T], U8, name="scale_table", align_bytes=64)
+        scale_table = keep.tile([P, T], U8, name="scale_table", align_bytes=DMA_ALIGN)
         nc.vector.memset(scale_table[:, 0 : T // 2].bitcast(I32), 0)
         nc.gpsimd.memset(scale_table[:, T // 2 : T].bitcast(I32), 0)
         nc.sync.dma_start(scale_table[:].bitcast(I32)[0:P:BLOCK_PARTITIONS, :], x_scales[0].bitcast(I32))
@@ -49,20 +50,20 @@ def tile_picked_ngramgate_none_po_kernel(
         nc.gpsimd.memset(warm_in[:], 0.0)
         nc.scalar.activation(warm_out[:], warm_in[:], SIGMOID)
 
-        x_planes = [keep.tile([P, S], U8, name="x_plane%d" % u, align_bytes=64) for u in range(2)]
+        x_planes = [keep.tile([P, S], U8, name="x_plane%d" % u, align_bytes=DMA_ALIGN) for u in range(2)]
         for plane in x_planes:
             nc.vector.memset(plane[:].bitcast(I32), 0)
 
         def load_weight(w, name):
-            raw = keep.tile([P, PACK, N], F32, name=name + "_raw", tag=name + "_raw")
+            raw = keep.tile([P, PACK, N], F32, name=name + "_raw", tag=name + "_raw", align_bytes=DMA_ALIGN)
             nc.sync.dma_start(raw[:], w.rearrange("(p j) c -> p j c", j=PACK))
             return raw
 
         nc.sync.dma_start(w3_raw[:, 1:PACK, :], w3_rows[:, 1:PACK, :])
-        word_table = keep.tile([P, T], I32, name="word_table", align_bytes=64)
+        word_table = keep.tile([P, T], I32, name="word_table", align_bytes=DMA_ALIGN)
         nc.sync.dma_start(word_table[:], x_words[0].rearrange("p c r -> p (c r)").bitcast(I32))
 
-        picked_scales = [keep.tile([P, S], U8, name="picked_scales%d" % u, align_bytes=64) for u in range(2)]
+        picked_scales = [keep.tile([P, S], U8, name="picked_scales%d" % u, align_bytes=DMA_ALIGN) for u in range(2)]
         nc.vector.tensor_copy(picked_scales[0][:], scale_table[:].indirect(offs_sb[:]))
         nc.vector.tensor_copy(picked_scales[1][:], scale_table[:].indirect(own_sb[:]))
 
@@ -80,15 +81,15 @@ def tile_picked_ngramgate_none_po_kernel(
 
         def quantize_weight(raw, name, vector_shares, pieces):
             src = raw[:].rearrange("p j (m t) -> p m j t", t=PACK)
-            pairs = [keep.tile([P, 2, P, PACK], BF16, name=name + "_bf16_%d" % u, align_bytes=64) for u in range(2)]
+            pairs = [keep.tile([P, 2, P, PACK], BF16, name=name + "_bf16_%d" % u, align_bytes=DMA_ALIGN) for u in range(2)]
             for u, share in enumerate(vector_shares):
                 dst = pairs[u][:].rearrange("p t m j -> p m j t")
                 if share < P:
                     nc.scalar.copy(dst[:, share:P], src[:, share:P, :, 2 * u : 2 * u + 2])
                 if share > 0:
                     nc.vector.tensor_copy(dst[:, 0:share], src[:, 0:share, :, 2 * u : 2 * u + 2])
-            codes = keep.tile([P, N], U32, name=name + "_codes", align_bytes=64)
-            scales = keep.tile([P, N], U8, name=name + "_scales", align_bytes=64)
+            codes = keep.tile([P, N], U32, name=name + "_codes", align_bytes=DMA_ALIGN)
+            scales = keep.tile([P, N], U8, name=name + "_scales", align_bytes=DMA_ALIGN)
             for t0, t1 in pieces:
                 cols = slice(t0 * P, t1 * P)
                 u = t0 // 2
@@ -113,8 +114,8 @@ def tile_picked_ngramgate_none_po_kernel(
 
         w3_mx = quantize_weight(w3_raw, "w3", (0, 88), ((0, 2), (2, 4)))
 
-        hashed_words = keep.tile([P, S], U32, name="hashed_words", align_bytes=64)
-        own_words = keep.tile([P, S], U32, name="own_words", align_bytes=64)
+        hashed_words = keep.tile([P, S], U32, name="hashed_words", align_bytes=DMA_ALIGN)
+        own_words = keep.tile([P, S], U32, name="own_words", align_bytes=DMA_ALIGN)
         nc.vector.tensor_copy(hashed_words[:], word_table[:].bitcast(U32).indirect(offs_sb[:]))
         nc.vector.tensor_copy(own_words[:], word_table[:].bitcast(U32).indirect(own_sb[:]))
 
@@ -122,7 +123,7 @@ def tile_picked_ngramgate_none_po_kernel(
         logits = []
 
         def make_gate(t, h0, h1, tag):
-            gate = keep.tile([P, (h1 - h0) * HALF], F32, name="gate%d_%d" % (t, h0), tag=tag)
+            gate = keep.tile([P, (h1 - h0) * HALF], F32, name="gate%d_%d" % (t, h0), tag=tag, align_bytes=DMA_ALIGN)
             nc.scalar.activation(gate[:], logits[t][:, h0 * HALF : h1 * HALF], SIGMOID)
             for h in range(h0, h1):
                 gates[h, t] = gate[:, (h - h0) * HALF : (h - h0 + 1) * HALF]
@@ -145,10 +146,10 @@ def tile_picked_ngramgate_none_po_kernel(
         sums[1, 3] = last_sums[:, HALF:S]
 
         w2_src = w2_raw[:].rearrange("p j (m t) -> p m j t", t=PACK)
-        w2_pairs = [keep.tile([P, 2, P, PACK], BF16, name="w2_bf16_%d" % u, align_bytes=64) for u in range(2)]
+        w2_pairs = [keep.tile([P, 2, P, PACK], BF16, name="w2_bf16_%d" % u, align_bytes=DMA_ALIGN) for u in range(2)]
         w2_mx = (
-            keep.tile([P, N], U32, name="w2_codes", align_bytes=64),
-            keep.tile([P, N], U8, name="w2_scales", align_bytes=64),
+            keep.tile([P, N], U32, name="w2_codes", align_bytes=DMA_ALIGN),
+            keep.tile([P, N], U8, name="w2_scales", align_bytes=DMA_ALIGN),
         )
 
         def round_w2(copy, u, m0, m1):
@@ -179,8 +180,8 @@ def tile_picked_ngramgate_none_po_kernel(
 
         out_run = out_0.rearrange("(p t) j -> p (t j)", t=PACK)
         out_words = out_1[0].rearrange("p c r -> p (c r)").bitcast(I32)
-        y_scales = keep.tile([P, S], U8, name="y_scales", align_bytes=64)
-        y_all = keep.tile([P, PACK * S], F32, name="y")
+        y_scales = keep.tile([P, S], U8, name="y_scales", align_bytes=DMA_ALIGN)
+        y_all = keep.tile([P, PACK * S], F32, name="y", align_bytes=DMA_ALIGN)
         y_rows = y_all[:].rearrange("p (t j) -> p t j", t=PACK)
         y = [y_rows[:, :, h * HALF : (h + 1) * HALF] for h in range(2)]
 
@@ -188,7 +189,7 @@ def tile_picked_ngramgate_none_po_kernel(
             run = slice(first * HALF, last * HALF)
             nc.sync.dma_start(out_run[:, run], y_all[:, run])
 
-        y_bf16 = [keep.tile([P, HALF, PACK], BF16, name="y%d_bf16" % h, align_bytes=64) for h in range(2)]
+        y_bf16 = [keep.tile([P, HALF, PACK], BF16, name="y%d_bf16" % h, align_bytes=DMA_ALIGN) for h in range(2)]
 
         def gate_sums(h, tiles, c0, c1):
             for t in tiles:
@@ -202,7 +203,7 @@ def tile_picked_ngramgate_none_po_kernel(
                 y[h][:, :, c0:c1].rearrange("p t (c i) -> p c t i", i=PACK),
             )
 
-        y_words = [keep.tile([P, HALF], U32, name="y%d_words" % h, align_bytes=64) for h in range(2)]
+        y_words = [keep.tile([P, HALF], U32, name="y%d_words" % h, align_bytes=DMA_ALIGN) for h in range(2)]
 
         def quantize_y(h, c0, c1):
             nc.vector.quantize_mx(
@@ -213,7 +214,7 @@ def tile_picked_ngramgate_none_po_kernel(
 
         quarter = HALF // 2
         for t in (1, 2):
-            staged = keep.tile([P, HALF], F32, name="staged%d" % t)
+            staged = keep.tile([P, HALF], F32, name="staged%d" % t, align_bytes=DMA_ALIGN)
             nc.scalar.copy(staged[:], sums[1, t])
             nc.gpsimd.tensor_tensor(y[1][:, t, :], staged[:], gates[1, t], MULT)
         gate_sums(0, (0,), 0, HALF)

@@ -21,6 +21,7 @@ QUADRANT = 32
 BLOCK_PARTITIONS = 8
 HALF = S // 2
 DMA_ALIGN = 256
+PAGE_ALIGN = 4096
 
 
 def tile_picked_ngramgate_none_po_kernel(
@@ -31,7 +32,7 @@ def tile_picked_ngramgate_none_po_kernel(
         keep = ctx.enter_context(tc.tile_pool(name="keep", bufs=1))
         psum = ctx.enter_context(tc.psum_pool(name="psum", bufs=1))
 
-        w3_raw = keep.tile([P, PACK, N], F32, name="w3_raw", align_bytes=DMA_ALIGN)
+        w3_raw = keep.tile([P, PACK, N], F32, name="w3_raw", align_bytes=PAGE_ALIGN)
         w3_rows = w3.rearrange("(p j) c -> p j c", j=PACK)
         nc.sync.dma_start(w3_raw[:, 0:1, :], w3_rows[:, 0:1, :])
 
@@ -40,7 +41,7 @@ def tile_picked_ngramgate_none_po_kernel(
         nc.sync.dma_start(offs_sb[:], offs)
         nc.sync.dma_start(own_sb[:], own)
 
-        scale_table = keep.tile([P, T], U8, name="scale_table", align_bytes=DMA_ALIGN)
+        scale_table = keep.tile([P, T], U8, name="scale_table", align_bytes=PAGE_ALIGN)
         nc.vector.memset(scale_table[:, 0 : T // 2].bitcast(I32), 0)
         nc.gpsimd.memset(scale_table[:, T // 2 : T].bitcast(I32), 0)
         nc.sync.dma_start(scale_table[:].bitcast(I32)[0:P:BLOCK_PARTITIONS, :], x_scales[0].bitcast(I32))
@@ -55,12 +56,12 @@ def tile_picked_ngramgate_none_po_kernel(
             nc.vector.memset(plane[:].bitcast(I32), 0)
 
         def load_weight(w, name):
-            raw = keep.tile([P, PACK, N], F32, name=name + "_raw", tag=name + "_raw", align_bytes=DMA_ALIGN)
+            raw = keep.tile([P, PACK, N], F32, name=name + "_raw", tag=name + "_raw", align_bytes=PAGE_ALIGN)
             nc.sync.dma_start(raw[:], w.rearrange("(p j) c -> p j c", j=PACK))
             return raw
 
         nc.sync.dma_start(w3_raw[:, 1:PACK, :], w3_rows[:, 1:PACK, :])
-        word_table = keep.tile([P, T], I32, name="word_table", align_bytes=DMA_ALIGN)
+        word_table = keep.tile([P, T], I32, name="word_table", align_bytes=PAGE_ALIGN)
         nc.sync.dma_start(word_table[:], x_words[0].rearrange("p c r -> p (c r)").bitcast(I32))
 
         picked_scales = [keep.tile([P, S], U8, name="picked_scales%d" % u, align_bytes=DMA_ALIGN) for u in range(2)]
@@ -123,7 +124,7 @@ def tile_picked_ngramgate_none_po_kernel(
         logits = []
 
         def make_gate(t, h0, h1, tag):
-            gate = keep.tile([P, (h1 - h0) * HALF], F32, name="gate%d_%d" % (t, h0), tag=tag, align_bytes=DMA_ALIGN)
+            gate = keep.tile([P, (h1 - h0) * HALF], F32, name="gate%d_%d" % (t, h0), tag=tag, align_bytes=PAGE_ALIGN if tag == "w2_raw" else DMA_ALIGN)
             nc.scalar.activation(gate[:], logits[t][:, h0 * HALF : h1 * HALF], SIGMOID)
             for h in range(h0, h1):
                 gates[h, t] = gate[:, (h - h0) * HALF : (h - h0 + 1) * HALF]
@@ -181,7 +182,7 @@ def tile_picked_ngramgate_none_po_kernel(
         out_run = out_0.rearrange("(p t) j -> p (t j)", t=PACK)
         out_words = out_1[0].rearrange("p c r -> p (c r)").bitcast(I32)
         y_scales = keep.tile([P, S], U8, name="y_scales", align_bytes=DMA_ALIGN)
-        y_all = keep.tile([P, PACK * S], F32, name="y", align_bytes=DMA_ALIGN)
+        y_all = keep.tile([P, PACK * S], F32, name="y", align_bytes=PAGE_ALIGN)
         y_rows = y_all[:].rearrange("p (t j) -> p t j", t=PACK)
         y = [y_rows[:, :, h * HALF : (h + 1) * HALF] for h in range(2)]
 
@@ -203,7 +204,7 @@ def tile_picked_ngramgate_none_po_kernel(
                 y[h][:, :, c0:c1].rearrange("p t (c i) -> p c t i", i=PACK),
             )
 
-        y_words = [keep.tile([P, HALF], U32, name="y%d_words" % h, align_bytes=DMA_ALIGN) for h in range(2)]
+        y_words = [keep.tile([P, HALF], U32, name="y%d_words" % h, align_bytes=PAGE_ALIGN) for h in range(2)]
 
         def quantize_y(h, c0, c1):
             nc.vector.quantize_mx(

@@ -117,22 +117,23 @@ def tile_picked_ngramgate_none_po_kernel(
 
         hashed_words = keep.tile([P, S], U32, name="hashed_words", align_bytes=DMA_ALIGN)
         own_words = keep.tile([P, S], U32, name="own_words", align_bytes=DMA_ALIGN)
-        nc.vector.tensor_copy(hashed_words[:], word_table[:].bitcast(U32).indirect(offs_sb[:]))
+        for h in range(2):
+            nc.vector.tensor_copy(
+                hashed_words[:, h * HALF : (h + 1) * HALF],
+                word_table[:].bitcast(U32).indirect(offs_sb[:, h * HALF // 16 : (h + 1) * HALF // 16]),
+            )
         nc.vector.tensor_copy(own_words[:], word_table[:].bitcast(U32).indirect(own_sb[:]))
 
         gates = {}
-        logits = []
-
-        def make_gate(t, h0, h1, tag):
-            gate = keep.tile([P, (h1 - h0) * HALF], F32, name="gate%d_%d" % (t, h0), tag=tag, align_bytes=PAGE_ALIGN if tag == "w2_raw" else DMA_ALIGN)
-            nc.scalar.activation(gate[:], logits[t][:, h0 * HALF : h1 * HALF], SIGMOID)
-            for h in range(h0, h1):
-                gates[h, t] = gate[:, (h - h0) * HALF : (h - h0 + 1) * HALF]
-
-        for t in range(PACK):
-            logits.append(psum.tile([P, S], F32, name="logits", tag="bank%d" % (PACK + t)))
-            product(logits[t][:], w3_mx, t, hashed_words, x_planes[0], 0, S, True, True)
-            make_gate(t, 0, 2 if t < PACK - 1 else 1, "gate%d" % t)
+        for h in range(2):
+            for u in range(2):
+                logits = psum.tile([P, 2, HALF], F32, name="logits", tag="bank%d" % (PACK + 2 * h + u))
+                for e in range(2):
+                    product(logits[:, e, :], w3_mx, 2 * u + e, hashed_words, x_planes[0], h * HALF, HALF, True, True)
+                gate = keep.tile([P, 2, HALF], F32, name="gate%d_%d" % (h, u), align_bytes=DMA_ALIGN)
+                nc.scalar.activation(gate[:], logits[:], SIGMOID)
+                for e in range(2):
+                    gates[h, 2 * u + e] = gate[:, e, :]
 
         w1_mx = quantize_weight(w1_raw, "w1", (P, P), ((0, 2), (2, 4)))
         sums = {}
@@ -165,16 +166,14 @@ def tile_picked_ngramgate_none_po_kernel(
                 in_=w2_pairs[t // 2][:, t % 2].rearrange("p m j -> p (m j)"),
             )
 
-        round_w2(nc.vector.tensor_copy, 0, 0, 84)
-        round_w2(nc.scalar.copy, 0, 84, P)
-        round_w2(nc.vector.tensor_copy, 1, 0, 36)
+        round_w2(nc.vector.tensor_copy, 0, 0, 88)
+        round_w2(nc.scalar.copy, 0, 88, P)
+        round_w2(nc.vector.tensor_copy, 1, 0, 72)
         round_w2(nc.scalar.copy, 1, 72, P)
         quantize_w2(0)
         quantize_w2(1)
-        round_w2(nc.vector.tensor_copy, 1, 36, 72)
         quantize_w2(2)
         quantize_w2(3)
-        make_gate(PACK - 1, 1, 2, "w2_raw")
         for h, t in ((0, 0), (1, 1), (1, 0), (0, 1), (0, 2), (1, 2)):
             product(sums[h, t], w2_mx, t, own_words, x_planes[1], h * HALF, HALF, False, True)
         product(last_sums[:], w2_mx, 3, own_words, x_planes[1], 0, S, False, True)

@@ -52,8 +52,7 @@ def tile_picked_ngramgate_none_po_kernel(
         nc.scalar.activation(warm_out[:], warm_in[:], SIGMOID)
 
         x_planes = [keep.tile([P, S], U8, name="x_plane%d" % u, align_bytes=DMA_ALIGN) for u in range(2)]
-        for plane in x_planes:
-            nc.vector.memset(plane[:].bitcast(I32), 0)
+        nc.vector.memset(x_planes[0][:].bitcast(I32), 0)
 
         def load_weight(w, name):
             raw = keep.tile([P, PACK, N], F32, name=name + "_raw", tag=name + "_raw", align_bytes=PAGE_ALIGN)
@@ -68,17 +67,19 @@ def tile_picked_ngramgate_none_po_kernel(
         nc.vector.tensor_copy(picked_scales[0][:], scale_table[:].indirect(offs_sb[:]))
         nc.vector.tensor_copy(picked_scales[1][:], scale_table[:].indirect(own_sb[:]))
 
-        def place_scale_rows(u):
-            for b in range(PACK):
+        nc.vector.tensor_copy(x_planes[1][:].bitcast(I32), picked_scales[1][:].bitcast(I32))
+
+        def place_scale_rows(u, first):
+            for b in range(first, PACK):
                 nc.sync.dma_start(
                     x_planes[u][:].bitcast(I32)[b:P:QUADRANT, :],
                     picked_scales[u][:].bitcast(I32)[b * BLOCK_PARTITIONS : P : QUADRANT, :],
                 )
 
-        place_scale_rows(0)
+        place_scale_rows(0, 0)
         w1_raw = load_weight(w1, "w1")
         w2_raw = load_weight(w2, "w2")
-        place_scale_rows(1)
+        place_scale_rows(1, 1)
 
         def quantize_weight(raw, name, vector_shares, pieces):
             src = raw[:].rearrange("p j (m t) -> p m j t", t=PACK)

from contextlib import ExitStack

import concourse.mybir as mybir

K, T, S, N = 512, 2048, 512, 512
FLOPS = 3 * 2 * K * N * S

F32 = mybir.dt.float32
BF16 = mybir.dt.bfloat16
I32 = mybir.dt.int32
U32 = mybir.dt.uint32
U16 = mybir.dt.uint16
U8 = mybir.dt.uint8
FP8X4 = mybir.dt.float8_e4m3fn_x4
SIGMOID = mybir.ActivationFunctionType.Sigmoid
MULT = mybir.AluOpType.mult

P = 128
PACK = 4
QUADRANT = 32
BLOCK_PARTITIONS = 8
HALF = S // 2
DMA_ALIGN = 256
PAGE_ALIGN = 4096


def tile_picked_ngramgate_none_po_kernel(
    tc, x_words, x_scales, w1, w2, w3, offs, own, out_0, out_1, out_2
):
    nc = tc.nc
    with ExitStack() as ctx:
        keep = ctx.enter_context(tc.tile_pool(name="keep", bufs=1))
        psum = ctx.enter_context(tc.psum_pool(name="psum", bufs=1))

        w3_raw = keep.tile([P, PACK, N], F32, name="w3_raw", align_bytes=PAGE_ALIGN)
        w3_rows = w3.rearrange("(p j) c -> p j c", j=PACK)
        nc.sync.dma_start(w3_raw[:, 0:1, :], w3_rows[:, 0:1, :])

        offs_sb = keep.tile([P, S // 16], U16, name="offs_sb", align_bytes=DMA_ALIGN)
        own_sb = keep.tile([P, S // 16], U16, name="own_sb", align_bytes=DMA_ALIGN)
        nc.sync.dma_start(offs_sb[:], offs)
        nc.sync.dma_start(own_sb[:], own)

        scale_table = keep.tile([P, T], U8, name="scale_table", align_bytes=PAGE_ALIGN)
        nc.vector.memset(scale_table[:, 0 : T // 2].bitcast(I32), 0)
        nc.gpsimd.memset(scale_table[:, T // 2 : T].bitcast(I32), 0)
        nc.sync.dma_start(scale_table[:].bitcast(I32)[0:P:BLOCK_PARTITIONS, :], x_scales[0].bitcast(I32))

        warm_in = keep.tile([P, 1], F32, name="warm_in")
        warm_out = keep.tile([P, 1], F32, name="warm_out")
        nc.gpsimd.memset(warm_in[:], 0.0)
        nc.scalar.activation(warm_out[:], warm_in[:], SIGMOID)

        x_planes = [keep.tile([P, S], U8, name="x_plane%d" % u, align_bytes=DMA_ALIGN) for u in range(2)]
        nc.vector.memset(x_planes[0][:].bitcast(I32), 0)

        def load_weight(w, name):
            raw = keep.tile([P, PACK, N], F32, name=name + "_raw", tag=name + "_raw", align_bytes=PAGE_ALIGN)
            nc.sync.dma_start(raw[:], w.rearrange("(p j) c -> p j c", j=PACK))
            return raw

        nc.sync.dma_start(w3_raw[:, 1:PACK, :], w3_rows[:, 1:PACK, :])
        word_table = keep.tile([P, T], I32, name="word_table", align_bytes=PAGE_ALIGN)
        nc.sync.dma_start(word_table[:], x_words[0].rearrange("p c r -> p (c r)").bitcast(I32))

        picked_scales = [keep.tile([P, S], U8, name="picked_scales%d" % u, align_bytes=DMA_ALIGN) for u in range(2)]
        nc.vector.tensor_copy(picked_scales[0][:], scale_table[:].indirect(offs_sb[:]))
        nc.vector.tensor_copy(picked_scales[1][:], scale_table[:].indirect(own_sb[:]))

        nc.vector.tensor_copy(x_planes[1][:].bitcast(I32), picked_scales[1][:].bitcast(I32))

        def place_scale_rows(u, first):
            for b in range(first, PACK):
                nc.sync.dma_start(
                    x_planes[u][:].bitcast(I32)[b:P:QUADRANT, :],
                    picked_scales[u][:].bitcast(I32)[b * BLOCK_PARTITIONS : P : QUADRANT, :],
                )

        place_scale_rows(0, 0)
        w1_raw = load_weight(w1, "w1")
        w2_raw = load_weight(w2, "w2")
        place_scale_rows(1, 1)

        def quantize_weight(raw, name, vector_shares, pieces):
            src = raw[:].rearrange("p j (m t) -> p m j t", t=PACK)
            pairs = [keep.tile([P, 2, P, PACK], BF16, name=name + "_bf16_%d" % u, align_bytes=DMA_ALIGN) for u in range(2)]
            for u, share in enumerate(vector_shares):
                dst = pairs[u][:].rearrange("p t m j -> p m j t")
                if share < P:
                    nc.scalar.copy(dst[:, share:P], src[:, share:P, :, 2 * u : 2 * u + 2])
                if share > 0:
                    nc.vector.tensor_copy(dst[:, 0:share], src[:, 0:share, :, 2 * u : 2 * u + 2])
            codes = keep.tile([P, N], U32, name=name + "_codes", align_bytes=DMA_ALIGN)
            scales = keep.tile([P, N], U8, name=name + "_scales", align_bytes=DMA_ALIGN)
            for t0, t1 in pieces:
                cols = slice(t0 * P, t1 * P)
                u = t0 // 2
                nc.vector.quantize_mx(
                    out=codes[:, cols].bitcast(FP8X4),
                    scales=scales[:, cols],
                    in_=pairs[u][:, t0 - 2 * u : t1 - 2 * u].rearrange("p t m j -> p (t m j)"),
                )
            return codes, scales

        def product(acc, weight, t, words, plane, c0, width, start, stop):
            codes, scales = weight
            nc.tensor.matmul_mx(
                out=acc,
                lhsT=codes[:, t * P : (t + 1) * P].bitcast(FP8X4),
                lhsT_scale=scales[:, t * P : (t + 1) * P],
                rhs=words[:, c0 : c0 + width].bitcast(FP8X4),
                rhs_scale=plane[:, c0 : c0 + width],
                start=start,
                stop=stop,
            )

        w3_mx = quantize_weight(w3_raw, "w3", (0, 88), ((0, 2), (2, 4)))

        hashed_words = keep.tile([P, S], U32, name="hashed_words", align_bytes=DMA_ALIGN)
        own_words = keep.tile([P, S], U32, name="own_words", align_bytes=DMA_ALIGN)
        for h in range(2):
            nc.vector.tensor_copy(
                hashed_words[:, h * HALF : (h + 1) * HALF],
                word_table[:].bitcast(U32).indirect(offs_sb[:, h * HALF // 16 : (h + 1) * HALF // 16]),
            )
        nc.vector.tensor_copy(own_words[:], word_table[:].bitcast(U32).indirect(own_sb[:]))

        gates = {}
        for h in range(2):
            for u in range(2):
                logits = psum.tile([P, 2, HALF], F32, name="logits", tag="bank%d" % (PACK + 2 * h + u))
                for e in range(2):
                    product(logits[:, e, :], w3_mx, 2 * u + e, hashed_words, x_planes[0], h * HALF, HALF, True, True)
                gate = keep.tile([P, 2, HALF], F32, name="gate%d_%d" % (h, u), align_bytes=DMA_ALIGN)
                nc.scalar.activation(gate[:], logits[:], SIGMOID)
                for e in range(2):
                    gates[h, 2 * u + e] = gate[:, e, :]

        w1_mx = quantize_weight(w1_raw, "w1", (P, P), ((0, 2), (2, 4)))
        sums = {}
        for h in range(2):
            for t in range(PACK - 1):
                bank = psum.tile([P, S], F32, name="sums", tag="bank%d" % (PACK * h + t))
                sums[h, t] = bank[:, 0:HALF]
                product(sums[h, t], w1_mx, t, hashed_words, x_planes[0], h * HALF, HALF, True, False)
        last_sums = psum.tile([P, S], F32, name="sums", tag="bank3")
        product(last_sums[:], w1_mx, 3, hashed_words, x_planes[0], 0, S, True, False)
        sums[0, 3] = last_sums[:, 0:HALF]
        sums[1, 3] = last_sums[:, HALF:S]

        w2_src = w2_raw[:].rearrange("p j (m t) -> p m j t", t=PACK)
        w2_pairs = [keep.tile([P, 2, P, PACK], BF16, name="w2_bf16_%d" % u, align_bytes=DMA_ALIGN) for u in range(2)]
        w2_mx = (
            keep.tile([P, N], U32, name="w2_codes", align_bytes=DMA_ALIGN),
            keep.tile([P, N], U8, name="w2_scales", align_bytes=DMA_ALIGN),
        )

        def round_w2(copy, u, m0, m1):
            dst = w2_pairs[u][:].rearrange("p t m j -> p m j t")
            copy(dst[:, m0:m1], w2_src[:, m0:m1, :, 2 * u : 2 * u + 2])

        def quantize_w2(t):
            cols = slice(t * P, (t + 1) * P)
            nc.vector.quantize_mx(
                out=w2_mx[0][:, cols].bitcast(FP8X4),
                scales=w2_mx[1][:, cols],
                in_=w2_pairs[t // 2][:, t % 2].rearrange("p m j -> p (m j)"),
            )

        round_w2(nc.vector.tensor_copy, 0, 0, 88)
        round_w2(nc.scalar.copy, 0, 88, P)
        round_w2(nc.vector.tensor_copy, 1, 0, 72)
        round_w2(nc.scalar.copy, 1, 72, P)
        quantize_w2(0)
        quantize_w2(1)
        quantize_w2(2)
        quantize_w2(3)
        for h, t in ((0, 0), (1, 1), (1, 0), (0, 1), (0, 2), (1, 2)):
            product(sums[h, t], w2_mx, t, own_words, x_planes[1], h * HALF, HALF, False, True)
        product(last_sums[:], w2_mx, 3, own_words, x_planes[1], 0, S, False, True)

        out_run = out_0.rearrange("(p t) j -> p (t j)", t=PACK)
        out_words = out_1[0].rearrange("p c r -> p (c r)").bitcast(I32)
        y_scales = keep.tile([P, S], U8, name="y_scales", align_bytes=DMA_ALIGN)
        y_all = keep.tile([P, PACK * S], F32, name="y", align_bytes=PAGE_ALIGN)
        y_rows = y_all[:].rearrange("p (t j) -> p t j", t=PACK)
        y = [y_rows[:, :, h * HALF : (h + 1) * HALF] for h in range(2)]

        def store_y(first, last):
            run = slice(first * HALF, last * HALF)
            nc.sync.dma_start(out_run[:, run], y_all[:, run])

        y_bf16 = [keep.tile([P, HALF, PACK], BF16, name="y%d_bf16" % h, align_bytes=DMA_ALIGN) for h in range(2)]

        def gate_sums(h, tiles, c0, c1):
            for t in tiles:
                nc.vector.tensor_tensor(
                    y[h][:, t, c0:c1], sums[h, t][:, c0:c1], gates[h, t][:, c0:c1], MULT
                )

        def round_y(copy, h, c0, c1):
            copy(
                y_bf16[h][:, c0:c1, :].rearrange("p (c i) t -> p c t i", i=PACK),
                y[h][:, :, c0:c1].rearrange("p t (c i) -> p c t i", i=PACK),
            )

        y_words = [keep.tile([P, HALF], U32, name="y%d_words" % h, align_bytes=PAGE_ALIGN) for h in range(2)]

        def quantize_y(h, c0, c1):
            nc.vector.quantize_mx(
                out=y_words[h][:, c0:c1].bitcast(FP8X4),
                scales=y_scales[:, h * HALF + c0 : h * HALF + c1],
                in_=y_bf16[h][:, c0:c1, :].rearrange("p c t -> p (c t)"),
            )

        quarter = HALF // 2
        for t in (1, 2):
            staged = keep.tile([P, HALF], F32, name="staged%d" % t, align_bytes=DMA_ALIGN)
            nc.scalar.copy(staged[:], sums[1, t])
            nc.gpsimd.tensor_tensor(y[1][:, t, :], staged[:], gates[1, t], MULT)
        gate_sums(0, (0,), 0, HALF)
        store_y(0, 1)
        gate_sums(1, (0,), 0, HALF)
        store_y(1, 2)
        gate_sums(0, (1,), 0, HALF)
        store_y(2, 3)
        gate_sums(0, (2, 3), 0, quarter)
        round_y(nc.scalar.copy, 0, 0, quarter)
        gate_sums(0, (2,), quarter, HALF)
        store_y(3, 5)
        gate_sums(0, (3,), quarter, HALF)
        round_y(nc.scalar.copy, 0, quarter, HALF)
        gate_sums(1, (3,), 0, HALF)
        store_y(5, 8)
        quantize_y(0, 0, quarter)
        round_y(nc.scalar.copy, 1, 192, HALF)
        round_y(nc.vector.tensor_copy, 1, 0, 192)
        quantize_y(0, quarter, HALF)
        nc.sync.dma_start(out_words[:, 0:HALF], y_words[0][:].bitcast(I32))
        quantize_y(1, 0, HALF)
        nc.sync.dma_start(out_words[:, HALF:S], y_words[1][:].bitcast(I32))

        for q in range(P // QUADRANT):
            queue = nc.scalar if q % 2 == 0 else nc.sync
            queue.dma_start(
                out_2[0, PACK * q : PACK * (q + 1), :].bitcast(I32),
                y_scales[:].bitcast(I32)[QUADRANT * q : QUADRANT * q + PACK, :],
            )
